import numpy as np, ml_dtypes
CORES = [113,118,241,246]
N = 4
BF = ml_dtypes.bfloat16
def gentries(a):
    return np.ascontiguousarray(a.reshape(8, 16, -1).transpose(0, 2, 1)).reshape(8, -1)
def gtable(e):
    e = np.asarray(e); return np.ascontiguousarray(e.reshape(8, -1, 16).transpose(0, 2, 1)).reshape(128, -1).astype(np.int32)
W, M, B, T, P, QU, TH = 2048, 512, 256, 4, 1, 12, 254
def parts(rng):
    d = {}
    d["pr"] = (224 * rng.random((N, 8, 1, W)) ** 3 + 32 * rng.random((N, 8, 16, W))).astype(np.int64)
    d["ad"] = (np.exp2(rng.integers(2, 8, (N, 8, 1, W))) * rng.random((N, 8, 16, W))).astype(np.int64)
    d["mc"] = rng.integers(0, W, (N, 8, 16, M))
    d["gl"] = (224 * rng.random((N, 8, 1, M)) + 32 * rng.random((N, 8, 16, M))).astype(np.int64)
    d["z"] = (224 * rng.random((N, 8, 1, B)) + 32 * rng.random((N, 8, 16, B))).astype(np.int64)
    d["m"] = rng.integers(0, M, (N, 8, B))
    d["dv"] = (np.exp2(rng.integers(2, 8, (N, 8, 1, T * P))) * rng.random((N, 8, 16, T * P))).astype(np.int64)
    d["wt"] = rng.integers(0, 256, (N, 8, 16, 1))
    return d
def flat(a):
    return np.ascontiguousarray(np.reshape(a, (N, 128, -1)))
def pack(d):
    h = {k: flat(d[k]).astype(np.float32).astype(BF) for k in ("pr", "ad", "gl", "z", "dv", "wt")}
    return {"pr": h["pr"], "ad": h["ad"], "mc": flat(d["mc"]).astype(np.int32), "gl": h["gl"], "z0": h["z"], "m0": np.stack([gtable(a) for a in d["m"]]), "dv": h["dv"], "wt": h["wt"]}
def setup_inputs(rng):
    return pack(parts(rng))
def sized(rng, hi, *shape):
    return np.minimum((float(hi + 1) ** rng.random(shape[:-2] + (1, shape[-1])) * rng.random(shape)).astype(np.int64), hi)
def setup_inputs_spread(rng):
    d = parts(rng)
    d["pr"] = sized(rng, 255, N, 8, 16, W); d["ad"] = sized(rng, 127, N, 8, 16, W); d["dv"] = sized(rng, 255, N, 8, 16, T * P); d["wt"] = sized(rng, 255, N, 8, 16, 1)
    a = sized(rng, 255, N, 8, 16, M); d["gl"] = np.where(rng.random((N, 8, 1, M)) < 0.5, 255 - a, a)
    a = sized(rng, 255, N, 8, 16, B); d["z"] = np.where(rng.random((N, 8, 1, B)) < 0.6, rng.integers(0, 256, (N, 8, 16, B)), a)
    d["mc"] = np.minimum((W * rng.random((N, 8, 16, M)) ** 3).astype(np.int64), W - 1)
    d["m"] = np.minimum((M * rng.random((N, 8, B)) ** 2).astype(np.int64), M - 1)
    return pack(d)
def mix(rng, hi, *shape):
    q = rng.choice(np.array([0.0, 0.1, 0.5, 0.8, 0.9, 1.0]), shape[:-2] + (1, shape[-1]))
    return (rng.random(shape) < q).astype(np.int64) * hi
def setup_inputs_ends(rng):
    d = {"pr": mix(rng, 255, N, 8, 16, W), "ad": mix(rng, 127, N, 8, 16, W), "mc": mix(rng, W - 1, N, 8, 16, M), "gl": mix(rng, 255, N, 8, 16, M), "z": mix(rng, 255, N, 8, 16, B),
         "m": (M - 1) * rng.integers(0, 2, (N, 8, B)), "dv": mix(rng, 255, N, 8, 16, T * P), "wt": mix(rng, 255, N, 8, 16, 1)}
    pr, ad, mc, gl, z, m, dv, wt = [d[k] for k in ("pr", "ad", "mc", "gl", "z", "m", "dv", "wt")]; a = N - 1
    wt[:, 0, :8] = 0; wt[:, 0, 8:] = 255
    gl[0, :, :, 0] = 0; gl[0, :, :, M - 1] = 0
    gl[1, :, :, 0] = 0; gl[1, :, :, M - 1] = 255; m[1] = 0; m[1, 7, B - 1] = M - 1; z[1, 7, :, B - 1] = 0; dv[1, 7, :, :P] = 0
    pr[a, 7, :, 0] = 255; ad[a, 7, :, 0] = 127; ad[a, 7, :, W - 1] = 0; gl[a, 7, :, 0] = 255; gl[a, 7, :, M - 1] = 255
    mc[a, 7, :, 0] = 0; mc[a, 7, :, M - 1] = W - 1
    wt[a, 7] = 0; wt[a, 7, 15] = 255; wt[a, 7, 13:15] = 1
    for i in (0, 1, B - 2, B - 1): z[a, 7, :, i] = 255
    m[a, 7, 1] = 0; m[a, 7, B - 2] = 0; m[a, 7, B - 1] = M - 1
    m[a, 7, :B - 1] = np.where(np.all(z[a, 7, 13:, :B - 1] == 255, axis=0), 0, m[a, 7, :B - 1])
    wt[a, 6] = 255; gl[a, 6, :, 0] = 0; z[a, 6, :, 0] = 255; z[a, 6, :, B - 1] = 255; z[a, 6, :, 1] = 0; z[a, 6, :, B - 2] = 0
    m[a, 6, 0] = 0; m[a, 6, 1] = 0; m[a, 6, B - 2] = 0; m[a, 6, B - 1] = M - 1
    return pack(d)
def setup_inputs_corners(rng):
    d = parts(rng); pr, ad, mc, gl, z, m, dv, wt = [d[k] for k in ("pr", "ad", "mc", "gl", "z", "m", "dv", "wt")]
    m[:, 0] = 0; m[:, 1] = M - 1; m[:, 2] = np.arange(B); m[:, 3] = M - 1 - np.arange(B)
    wt[:, 0] = 0; wt[:, 1] = 255; dv[:, 4] = 255; dv[:, 5] = 0
    one = rng.integers(0, W, (N, 1, M)); one[:, 0, 0] = 0; one[:, 0, M - 1] = W - 1; mc[:, 4] = one; m[:, 4, 0] = 0; m[:, 4, B - 1] = M - 1
    gl[:, 5] = np.maximum(gl[:, 5], 1); goal = np.take_along_axis(gl[:, 5], m[:, 5][:, None, :], 2)
    c = rng.choice(np.array([0, QU - 1, QU, QU + 1, 16]), (N, 1, B)); place = np.argsort(np.argsort(rng.random((N, 16, B)), axis=1), axis=1)
    z[:, 5] = goal - (place >= c)
    ad[:, 6] = TH // 16; ad[:, 6, 15] = TH - 15 * (TH // 16) + rng.integers(-1, 2, (N, W))
    pr[:, 6] = np.maximum(pr[:, 6], 40); gl[:, 6] = np.maximum(gl[:, 6], 200); z[:, 6] = np.where(rng.random((N, 1, B)) < 0.7, 255, z[:, 6])
    pr[:, 7] = 255; gl[:, 7] = 255; z[:, 7] = 255 * rng.integers(0, 2, (N, 1, B)); wt[:, 7] = (255 * (np.arange(N) & 1)).reshape(N, 1, 1)
    return pack(d)
def setup_inputs_crowd(rng):
    d = parts(rng); pr, gl, z, m, dv, wt = [d[k] for k in ("pr", "gl", "z", "m", "dv", "wt")]
    gl[:, :6] = 0; m[:, :4] = np.argsort(rng.random((N, 4, M)), axis=-1)[..., :B]
    wt[:, :4] = 0; wt[:, :4, 0] = 1; wt[:, :4, 1] = 255
    c = np.full((N, 4, B), M - 1); c[:, 1, 0] = 0; c[:, 3] = rng.choice(np.array([0, 1, M // 2, M - 1]), (N, B))
    v = (c - 37 * m[:, :4]) & (M - 1); z[:, :4, 0] = v - 255 * (v // 255); z[:, :4, 1] = v // 255
    for i in range(N): gl[i, 2, :, m[i, 2, 0]] = 255
    z[:, 2, 2:, 0] = 100; dv[:, 2, :, :P] = 1
    for g in (4, 5):
        z[:, g] = z[:, g, :, :1].copy(); m[:, g] = m[:, g, :1].copy()
    z[:, 5, :, B - 1] = 255 - z[:, 5, :, 0]
    gl[:, 6] = 255
    pr[:, 7] = 255; gl[:, 7] = 255; z[:, 7] = 0; z[:, 7, :, B - 1] = 255; m[:, 7] = m[:, 7, :1].copy()
    return pack(d)
def setup_inputs_few(rng):
    d = parts(rng); d["z"] = np.minimum(d["z"], 254); d["dv"] = np.maximum(d["dv"], 1)
    mc, gl, z, m, wt = [d[k] for k in ("mc", "gl", "z", "m", "wt")]
    gl[1::2] = 255; z[1::2, 7, :, B - 1] = 255
    full = rng.permutation(np.array([0, 1, 3, 4]))
    for i in range(0, N, 2):
        g = int(full[(i // 2) & 3]); gl[i, g] = 0; m[i, g] = rng.permutation(M)[:B]
        wt[i, g] = 0; wt[i, g, 0] = 1; wt[i, g, 1] = 255
        a = rng.choice(np.array([11, 13, 23, 25, 27, 29]), B); u = W - 32 + a
        z[i, g, 1] = u // 255; z[i, g, 0] = u - 255 * (u // 255)
        mc[i, g, 15, m[i, g]] = W - 32 + ((-(a ** 7)) & 31)
    return pack(d)
def check_inputs(d):
    bad = []
    for k, hi in (("pr", 255), ("ad", 127), ("mc", W - 1), ("gl", 255), ("z0", 255), ("m0", M - 1), ("dv", 255), ("wt", 255)):
        a = np.asarray(d[k]).astype(np.float64)
        if not (np.min(a) >= 0 and np.max(a) <= hi): bad.append("range of " + k)
        elif np.any(a != np.floor(a)): bad.append("whole numbers of " + k)
    return bad
def reference(pr, ad, mc, gl, z0, m0, dv, wt):
    need_of, add_of, goal_of, z, dist, weight = [a.astype(np.float32).astype(np.int64).reshape(N, 8, 16, -1) for a in (pr, ad, gl, z0, dv, wt)]
    tb = mc.astype(np.int64).reshape(N, 8, 16, M); m = np.stack([gentries(a) for a in m0]).astype(np.int64)
    seen = [0] * N
    for t in range(T):
        for q in range(N):
            s = (q - t) % N; zz = z[s]; mm = m[s]
            o = np.take_along_axis(tb[q], mm[:, None, :], 2)
            ix = o.reshape(8, 1, 16 * B)
            p = np.take_along_axis(need_of[q], ix, 2).reshape(8, 16, 16, B); a = np.take_along_axis(add_of[q], ix, 2).reshape(8, 16, 16, B)
            K = [None] * 16 + [np.take_along_axis(goal_of[q], mm[:, None, :], 2)]
            for k in range(15, -1, -1): K[k] = np.maximum(p[:, :, k], K[k + 1] - a[:, :, k])
            K = np.stack(K)
            for j in range(P):
                met = np.add.reduce((zz[None] >= K).astype(np.int64), axis=2)
                best = np.max(np.where(met >= QU + (seen[q] & 1), np.arange(17).reshape(17, 1, 1), -1), axis=0)
                ak = np.take_along_axis(a, np.clip(best, 0, 15)[:, None, None, :], 2)[:, :, 0]
                new = np.abs(np.minimum(255, zz + ak) - dist[q, :, :, t * P + j][:, :, None])
                zz = np.where(((best >= 0) & (best < 16))[:, None, :], new, zz)
            goal = best == 16
            u = np.add.reduce(weight[q] * zz, axis=1) & (W - 1); to = (u + 37 * mm) & (M - 1)
            use = np.add.reduce(np.minimum(a, K[1:].transpose(1, 2, 0, 3)), axis=1)
            fresh = (((o * u[:, None, :]) >> 5) + o + 37 * np.arange(16).reshape(1, 16, 1)) & (W - 1)
            o = np.where(use < TH, fresh, o)
            for g in range(8):
                who = np.flatnonzero(goal[g]); where, first = np.unique(to[g, who], return_index=True)
                tb[q, g][:, where] = o[g][:, who[first]]
            z[s] = zz; m[s] = np.where(goal | (best < 0), to, mm); seen[q] = int(np.count_nonzero(goal))
    back = [(q - (T - 1)) % N for q in range(N)]
    return {"ymc": tb.reshape(N, 128, M).astype(np.float32), "yz": z[back].reshape(N, 128, B).astype(np.float32), "ym": np.stack([gtable(m[s]) for s in back]).astype(np.float32)}

@@ -1,0 +1,505 @@
+from concourse.mybir import dt, AluOpType, AxisListType, ActivationFunctionType
+A = AluOpType
+F = ActivationFunctionType
+
+T_STEPS, W, M, B, QU, TH = 4, 2048, 512, 256, 12, 254
+BIG = 131072.0
+HALF = [(0, 128), (128, 256)]
+VPR = [16, 0]
+CMPV = ["VVVV", "VSSS"]
+ORDER = ("GB:0 prs:0 o16:1 ml prv:0 GB:1 zs gw:0 c16 prs:1 scan:0 grep xq bit ble blo br use:0 toL d0:3 d0:2 glt of ad:1 prv:1 d0:1 d0:0 ui fl "
+         "ok:0 gw:1 oh:0 p0 p1 vl:0 scan:1 p2 dl:0 t1:0 p3 oP p4 p5 t2:0 use:1 sm:0 uu td conf fq ft d1:3 t3:0 sz:0 fr d1:2 low df ldf cx wr "
+         "+o16:0 d1:1 +ad:0 d1:0 fl ok:1 oh:1 vl:1 dl:1 t1:1 as t2:1 sm:1 t3:1 par sz:1").split()
+SB, PS = "sbuf", "psum"
+BF, F4, I4, U2 = "bfloat16", "float32", "int32", "uint16"
+SCRATCH = {"CMP": (SB, [128, B, 16], BF), "EQ0": (SB, [128, 16, 128], BF), "EQ1": (SB, [128, 8, 128], BF),
+           "bD0": (PS, [128, 128, 4], F4), "bD1": (PS, [128, 128, 4], F4), "bG0": (PS, [128, 16, 32], F4), "bG1": (PS, [128, 16, 32], F4)}
+for _n, _w, _d in ([(x, 512, F4) for x in ("bM", "bL", "bF", "bO")]
+                   + [("PRW", W, BF), ("ADW", W, BF), ("GLW", M, BF), ("MCI", M, I4), ("MC", M + B, F4), ("WI", M, I4), ("WJI", M, I4), ("W37", M, BF),
+                      ("M0", 16, I4), ("DV", 4, BF), ("WT", 1, BF), ("O16", B, U2), ("D0", 32 * B, BF), ("D1", 32 * B, BF), ("KR", 32 * B, BF),
+                      ("AOFF", 16, U2), ("OFF", 16, U2), ("GLT", 32, BF), ("CX", 128, F4), ("LI", 64, I4), ("LF", 144, F4), ("CI", 4, I4),
+                      ("CF", 24, F4), ("THR", 8, F4), ("AI", 2, I4), ("DG", 512, BF), ("DT", 512, BF), ("IOT", B, F4), ("TB", 64, F4), ("SL", 48, F4), ("B32", 8, BF)]
+                   + [(x, 144, BF) for x in ("E1", "E2", "E0", "EH", "NE", "WE", "WJ")]
+                   + [(x, B, BF) for x in ("GB", "MB", "C16", "P0", "BLE", "BLO", "BR", "GREP", "OK", "OH")]
+                   + [(x, B, I4) for x in ("UI", "UU", "FQ", "FT", "FR", "XQ", "BIT")]
+                   + [(x, B, F4) for x in ("OF", "DF", "LDF", "T1", "T2", "T3", "ZF")]
+                   + [(x, 128, F4) for x in ("DX1", "DX2", "DX")]
+                   + [(x, 128, BF) for x in ("ONE", "BO1", "BO", "IDN", "NID", "NBO", "U1", "UP", "NEG", "BW")]):
+    SCRATCH[_n] = (PS if _n in ("bM", "bL", "bF", "bO") else SB, [128, _w], _d)
+LOADS = ["m0", "mc", "z0", "gl", "wt", "dv", "pr", "ad"]
+OUTS = ["ymc", "yz0", "yz1", "ym"]
+SEMAPHORES = ["V", "S", "T", "G"] + ["l_" + n for n in LOADS] + ["o_" + n for n in OUTS]
+for _t in range(T_STEPS):
+    SCRATCH["Z%d" % _t] = (SB, [128, B], BF)
+    SCRATCH["ML%d" % _t] = (SB, [128, 16], U2)
+    if _t:
+        SCRATCH["ZO%d" % _t] = (SB, [128, B], BF)
+        SCRATCH["MO%d" % _t] = (SB, [128, 16], U2)
+        SEMAPHORES += ["%s%s%d%d" % (a, b, _t, h) for a in "rs" for b in "mz" for h in (0, 1)]
+
+
+def rank_program(g, core, T, topo):
+    rank = T.rank_of(core)
+    if rank is None:
+        return
+    n = len(T.cores)
+    nxt, prv = T.cores[(rank + 1) % n], T.cores[(rank - 1) % n]
+    V, S, P = g.vector, g.scalar, g.tensor
+    QS = {"V": V, "S": S, "T": P, "G": g, "Y": g.sync}
+    cnt = {e: 0 for e in QS}
+    clock = {e: {} for e in QS}
+    snap = {}
+    wrote, read, bank = {}, {}, {}
+
+    def need(e, pairs):
+        want = {}
+        for s, v in pairs:
+            want[s] = max(want.get(s, 0), v)
+        for s, v in want.items():
+            if clock[e].get(s, 0) < v:
+                QS[e].wait_ge(T.sem[s], v)
+                clock[e][s] = v
+                for s2, v2 in snap.get((s, v), {}).items():
+                    clock[e][s2] = max(clock[e].get(s2, 0), v2)
+
+    def deps(e, r, w, b):
+        p = [wrote[x] for x in r]
+        for x in w:
+            q = ([wrote[x]] if x in wrote else []) + list(read.get(x, {}).items())
+            p += [y for y in q if not (e == "T" and y[0] == "T")]
+        for x in b:
+            p += [q for q in bank.get(x, {}).items() if q[0] != e]
+        need(e, p)
+
+    def mark(tag, r, w, b):
+        for x in r:
+            d = read.setdefault(x, {})
+            d[tag[0]] = max(d.get(tag[0], 0), tag[1])
+        for x in w:
+            wrote[x] = tag
+            read[x] = {}
+        for x in b:
+            bank.setdefault(x, {})[tag[0]] = tag[1]
+
+    def op(e, fn, r="", w="", b=""):
+        r, w, b = r.split(), w.split(), b.split()
+        deps(e, r, w, b)
+        cnt[e] += 1
+        fn().then_inc(T.sem[e], 1)
+        snap[(e, cnt[e])] = dict(clock[e])
+        mark((e, cnt[e]), r, w, b)
+
+    def dma(e, out, in_, sem, r="", w=""):
+        r, w = r.split(), w.split()
+        deps(e, r, w, [])
+        QS[e].dma_start(out, in_).then_inc(T.sem[sem], 16)
+        mark((sem, 16), r, w, [])
+
+    eng = lambda a, b: topo.engines(a, b)[:8]
+
+    def send(buf, t, h, c0, c1, src, r):
+        rid, pid = topo.addr(nxt, core)
+        deps("G", [r], [], [])
+        k = ("m" if buf == "ML" else "z") + "%d%d" % (t, h)
+        g.remote_dma(T[buf + str(t)][:, c0:c1], src[:, c0:c1], T.sem["r" + k], T.sem["s" + k], pid, rid, sum(1 << e for e in eng(core, nxt)))
+        mark(("s" + k, len(eng(core, nxt))), [r], [], [])
+        wrote["%s%d_%d" % (buf, t, h)] = ("r" + k, len(eng(prv, core)))
+
+    def mm(out, l, rr, r, w, b, st=True, sp=True):
+        op("T", lambda: P.matmul(out, l, rr, st, sp), r, w, b)
+
+    def tt(out, a, c, o, r, w, b=""):
+        op("V", lambda: V.tensor_tensor(out, a, c, o), r, w, b)
+
+    def ts(out, a, s1, s2, o1, o2, r, w, b=""):
+        if o2 is None:
+            op("V", lambda: V.tensor_scalar(out, a, s1, None, o1), r, w, b)
+        else:
+            op("V", lambda: V.tensor_scalar(out, a, s1, s2, o1, o2), r, w, b)
+
+    def tc(out, a, r, w, b=""):
+        op("V", lambda: V.tensor_copy(out, a), r, w, b)
+
+    def ms(out, c, w):
+        op("V", lambda: V.memset(out, c), "", w)
+
+    def act(out, a, f, r, w, b="", **kw):
+        op("S", lambda: S.activation(out, a, f, **kw), r, w, b)
+
+    def aff(o, i, pat, cmp, fill, base, cm, r, w):
+        op("G", lambda: g.affine_select(o[:], i[:], pat, cmp, fill, base, cm), r, w)
+
+    def slot(pad, k):
+        return pad[:, 15 - k:143 - k]
+
+    cf = lambda i: T.CF[:, i:i + 1]
+    li = lambda i: T.LI[:, 16 * i:16 * i + 16]
+    lf = lambda i: T.LF[:, 16 * i:16 * i + 16]
+    lh = lambda i, h: T.LF[:, 16 * i + 8 * h:16 * i + 8 * h + 8]
+    L = lambda i: T.bL[:, i:i + 16]
+
+    dma("Y", T.M0[:], T.m0[:], "l_m0", "", "M0")
+    dma("Y", T.MCI[:], T.mc[:], "l_mc", "", "MCI")
+    dma("S", T.GLW[:], T.gl[:], "l_gl", "", "GLW")
+    dma("S", T.ADW[:], T.ad[:], "l_ad", "", "ADW")
+    dma("Y", T.PRW[:], T.pr[:], "l_pr", "", "PRW")
+    dma("Y", T.Z0[:], T.z0[:], "l_z0", "", "Z0_0 Z0_1")
+    dma("Y", T.WT[:], T.wt[:], "l_wt", "", "WT")
+    dma("Y", T.DV[:], T.dv[:], "l_dv", "", "DV")
+
+    ms(T.ONE[:], 1.0, "ONE")
+    ms(T.E1[:], 0.0, "E1")
+    ms(T.E1[:, 15::16], 1.0, "E1")
+    op("G", lambda: g.iota(T.CI[:, 0:1], [[0, 1]], 0, 1), "", "pc")
+    op("G", lambda: g.iota(T.IOT[:], [[1, B]], 0, 0, allow_small_or_imprecise_dtypes=True), "", "IOT")
+    aff(T.E2, T.E1, [[-16, 9], [0, 16]], A.is_ge, 0.0, 0, 1, "E1", "E2")
+    aff(T.E0, T.E2, [[16, 9], [0, 16]], A.is_ge, 0.0, 15, -1, "E2", "E0")
+    aff(T.BO1, T.ONE, [[-16, 8], [0, 16]], A.is_ge, 0.0, 0, 1, "ONE", "BO1")
+    aff(T.BO, T.BO1, [[16, 8], [0, 16]], A.is_ge, 0.0, 15, -1, "BO1", "BO")
+    aff(T.IDN, T.ONE, [[-1, 128]], A.is_equal, 0.0, 0, 1, "ONE", "IDN")
+    op("G", lambda: g.iota(T.WI[:], [[37, M]], 0, 0), "", "WI")
+    ts(T.CI[:, 1:2], T.CI[:, 0:1], 15, None, A.bitwise_and, None, "pc", "kc")
+    ts(T.CI[:, 2:3], T.CI[:, 0:1], 4, None, A.arith_shift_right, None, "pc", "gc")
+    ts(T.CI[:, 3:4], T.CI[:, 0:1], 4, 1, A.arith_shift_right, A.bitwise_and, "pc", "oc")
+    ms(T.TB[:, 0:16], 0.5, "tba")
+    ms(T.TB[:, 16:32], 0.0, "tbb")
+    tc(cf(0), T.CI[:, 1:2], "kc", "kf")
+    tc(cf(1), T.CI[:, 2:3], "gc", "gf")
+    tc(cf(2), T.CI[:, 3:4], "oc", "odd")
+    tc(cf(3), T.CI[:, 0:1], "pc", "pf")
+    op("V", lambda: V.tensor_tensor_scan(T.TB[:, 32:48], T.TB[:, 0:16], T.TB[:, 16:32], 2.0, A.mult, A.add), "tba tbb", "tbc")
+    ts(cf(5), cf(0), 8.5, None, A.is_le, None, "kf", "le8")
+    ts(cf(6), cf(0), 9.0, None, A.is_equal, None, "kf", "is9")
+    ts(T.TB[:, 48:64], T.IOT[:, 0:16], cf(0), None, A.is_equal, None, "IOT kf", "tbm")
+    ts(cf(4), cf(2), -1.0, 1.0, A.mult, A.add, "odd", "even")
+    ts(cf(7), cf(5), -0.5, cf(6), A.mult, A.add, "le8 is9", "base")
+    ts(cf(12), cf(6), 2.0 ** -9, None, A.mult, None, "is9", "c9")
+    ts(cf(13), cf(5), -0.5, None, A.mult, None, "le8", "nle8")
+    tt(T.TB[:, 0:16], T.TB[:, 32:48], T.TB[:, 48:64], A.mult, "tbc tbm", "tba")
+    tc(T.ML0[:], T.M0[:], "M0", "ML0_0 ML0_1")
+    ms(T.MC[:, M:M + B], 0.0, "MC")
+    tc(T.MC[:, 0:M], T.MCI[:], "MCI", "MC")
+
+    def later_const():
+        ts(T.NID[:], T.IDN[:], -1.0, None, A.mult, None, "IDN", "NID")
+        ts(T.BW[:], T.BO[:], T.WT[:, 0:1], None, A.mult, None, "BO WT", "BW")
+        ts(T.WE[:], T.E0[:], T.WT[:, 0:1], None, A.mult, None, "E0 WT", "WE")
+        ts(T.WJI[:], T.WI[:], M - 1, None, A.bitwise_and, None, "WI", "WJI")
+        ms(cf(21), 0.5, "half")
+        ms(cf(22), 255.0, "c255")
+        ms(cf(23), -255.0, "cm255")
+        ms(T.THR[:, 0:1], float(2 * QU - 16), "thd0")
+        ms(T.THR[:, 4:5], 17.0 - 2 * QU, "thb0")
+        ts(T.W37[:], T.WJI[:], -256.0, None, A.add, None, "WJI", "W37")
+        op("V", lambda: V.tensor_reduce(cf(14), T.TB[:, 0:16], AxisListType.X, A.add), "tba", "cb0")
+        ts(cf(8), cf(5), cf(4), None, A.mult, None, "le8 even", "e1")
+        ts(cf(9), cf(7), cf(4), None, A.mult, None, "base even", "e2")
+        ts(cf(10), cf(5), cf(2), None, A.mult, None, "le8 odd", "o1")
+        ts(cf(11), cf(7), cf(2), None, A.mult, None, "base odd", "o2")
+        ts(T.bM[:, B:2 * B], T.IOT[:], cf(12), cf(13), A.mult, A.add, "IOT c9 nle8", "CONST", "bM")
+        ts(cf(15), cf(14), cf(5), None, A.mult, None, "cb0 le8", "cb")
+        ts(cf(5), cf(14), 0.5, -0.5, A.mult, A.add, "cb0 cb", "cb2 le8")
+        ts(cf(16), cf(0), 1184.0, None, A.mult, None, "kf", "c1184")
+        ts(cf(17), cf(0), 2.0, -1.0, A.mult, A.add, "kf", "cj")
+        ts(cf(18), cf(1), -BIG, 7 * BIG + 0.5, A.mult, A.add, "gf", "nb")
+        ts(cf(19), cf(3), -1.0, -1152.0, A.mult, A.add, "pf", "bias0")
+        ts(cf(20), cf(3), -1.0, -1280.0, A.mult, A.add, "pf", "bias1")
+        ts(T.SL[:, 32:48], T.IOT[:, 0:16], 16.0, cf(0), A.mult, A.add, "IOT kf", "sl")
+        ms(T.DX1[:], -16.0 * BIG, "DX1")
+        ts(T.NBO[:], T.BO[:], -1.0, None, A.mult, None, "BO", "NBO")
+        ts(T.NEG[:], T.BO[:], -0.03125, None, A.mult, None, "BO", "NEG")
+        ts(T.NE[:], T.E0[:], -1.0, None, A.mult, None, "E0", "NE")
+        ts(T.EH[:], T.E0[:], 2.0, None, A.mult, None, "E0", "EH")
+        ts(T.WJ[:], T.E0[:], cf(17), None, A.mult, None, "E0 cj", "WJ")
+        ts(T.SL[:, 0:16], T.SL[:, 32:48], 32.0, None, A.mult, None, "sl", "b32f")
+        ts(T.SL[:, 16:32], T.SL[:, 32:48], float(M), None, A.add, None, "sl", "b512")
+        tc(T.B32[:], T.SL[:, 0:8], "b32f", "B32")
+        aff(T.U1, T.NBO, [[-1, 128]], A.not_equal, 1.0, 0, 1, "NBO", "U1")
+        aff(T.UP, T.U1, [[-1, 128]], A.is_ge, 0.0, 0, 1, "U1", "UP")
+        aff(T.DX2, T.DX1, [[0, 16], [-16, 8]], A.is_ge, BIG, 0, 1, "DX1", "DX2")
+        aff(T.DX, T.DX2, [[0, 16], [16, 8]], A.is_ge, BIG, 15, -1, "DX2", "DX")
+
+    def zeros(c):
+        s0, s1 = HALF[c]
+        ms(T.D0[:, 32 * s0:32 * s1:2], 0.0, "d0z%d" % c)
+        ms(T.D0[:, 32 * s0:32 * s1:32], -512.0, "d0z%d" % c)
+        ms(T.D1[:, 32 * s0 + 1:32 * s1:2], 0.0, "d1z%d" % c)
+
+    def passes():
+        for t in range(T_STEPS):
+            ts(T.DG[:, 128 * t:128 * t + 128], T.IDN[:], T.DV[:, t:t + 1], None, A.mult, None, "IDN DV", "DG%d" % t)
+        mm(T.bF[:], T.BO[:], T.DG[:], "BO DG0 DG1 DG2 DG3", "dtp", "bF")
+        tc(T.DT[:], T.bF[:], "dtp", "DT", "bF")
+
+    def step(t):
+        last = t == T_STEPS - 1
+        Z, ML = T["Z%d" % t], T["ML%d" % t]
+        zh, mh = ["Z%d_0" % t, "Z%d_1" % t], ["ML%d_0" % t, "ML%d_1" % t]
+        zr, mr, thd = " ".join(zh), " ".join(mh), "thd%d" % t
+        thdc = T.THR[:, t:t + 1]
+        pend = []
+        for x in ("d1v0", "d1v1", "d1s0", "d1s1"):
+            wrote.setdefault(x, ("V", 1))
+
+        def kr(c, i):
+            return T.KR[:, 32 * HALF[c][0] + i:32 * HALF[c][1]:32]
+
+        def o16(c):
+            s0, s1 = HALF[c]
+            tc(T.O16[:, s0:s1], T.MC[:, 0:M].indirect(ML[:, 8 * c:8 * c + 8]), "MC " + mh[c], "O16%d" % c)
+
+        def GB(c):
+            s0, s1 = HALF[c]
+            act(T.GB[:, s0:s1], T.GLW[:].indirect(ML[:, 8 * c:8 * c + 8]), F.Copy, "GLW " + mh[c], "GB%d" % c)
+
+        def ad(c):
+            s0, s1 = HALF[c]
+            act(T.D0[:, 32 * s0 + 1:32 * s1:2], T.ADW[:].indirect(T.O16[:, s0:s1]), F.Copy, "ADW O16%d" % c, "d0a%d" % c, scale=-1.0)
+
+        def prs(c):
+            s0, s1 = HALF[c]
+            s0 += VPR[c]
+            if s1 > s0:
+                act(T.D1[:, 32 * s0:32 * s1:2], T.PRW[:].indirect(T.O16[:, s0:s1]), F.Copy, "PRW O16%d" % c, "d1s%d" % c)
+
+        def prv_(c):
+            s0 = HALF[c][0]
+            s1 = s0 + VPR[c]
+            if s1 > s0:
+                tc(T.D1[:, 32 * s0:32 * s1:2], T.PRW[:].indirect(T.O16[:, s0:s1]), "PRW O16%d" % c, "d1v%d" % c)
+
+        def gw(c):
+            s0, s1 = HALF[c]
+            if t == 0:
+                zeros(c)
+            tc(T.P0[:, s0:s1], T.D1[:, 32 * s0:32 * s1:32], "d1v%d d1s%d" % (c, c), "P0%d" % c)
+            tc(T.D1[:, 32 * s0 + 32:32 * s1:32], T.GB[:, s0:s1 - 1], "GB%d" % c, "d1v%d d1s%d" % (c, c))
+
+        def scan(c):
+            s0, s1 = HALF[c]
+            hi, lo = 32 * s1 - 1, 32 * s0 - 1 if s0 else None
+            op("V", lambda: V.tensor_tensor_scan(T.KR[:, hi:lo:-1], T.D0[:, hi:lo:-1], T.D1[:, hi:lo:-1], T.GB[:, s1 - 1:s1], A.add, A.max),
+               "GB{0} d0a{0} d0z{0} d1v{0} d1s{0} d1z{0}".format(c), "KR%d" % c)
+            tt(kr(c, 0), T.P0[:, s0:s1], kr(c, 1), A.max, "P0%d KR%d" % (c, c), "K0%d" % c)
+
+        def diff(c, q):
+            s0, s1 = HALF[c]
+            bn = "bD%d" % (q & 1)
+            bd = T[bn]
+            e = CMPV[c][q]
+            for j in range(4):
+                mm(bd[:, :, j], T.NID[:], kr(c, 8 * q + 2 * j), "NID KR%d K0%d" % (c, c), bn, bn, True, False)
+                mm(bd[:, :, j], T.IDN[:], Z[:, s0:s1], "IDN " + zh[c], bn, bn, False, True)
+            name = "cmp%d%d" % (c, q)
+            if e == "S":
+                act(T.CMP[:, s0:s1, 4 * q:4 * q + 4], bd[:], F.Sign, bn + " half", name, bn, bias=cf(21))
+            else:
+                ts(T.CMP[:, s0:s1, 4 * q:4 * q + 4], bd[:], 0.0, 0.5, A.is_ge, A.subtract, bn, name, bn)
+            flush()
+            pend.append((c, q, e, name))
+
+        def flush():
+            for c, q, e, name in pend:
+                s0, s1 = HALF[c]
+                for k in range(4 * q + 3, 4 * q - 1, -1):
+                    mm(T.bM[:, s0:s1], slot(T.E0 if e == "S" else T.EH, k), T.CMP[:, s0:s1, k], "E0 EH " + name, "met%d" % c, "bM", k == 15, k == 0)
+            del pend[:]
+
+        def use(c):
+            s0, s1 = HALF[c]
+            for k in range(15, -1, -1):
+                up = kr(c, 2 * k + 2) if k < 15 else T.GB[:, s0:s1]
+                mm(T.bL[:, B + s0:B + s1], slot(T.E0, k), up, "E0 GB%d KR%d" % (c, c), "use%d" % c, "bL", k == 15, False)
+                mm(T.bL[:, B + s0:B + s1], slot(T.NE, k), kr(c, 2 * k + 1), "NE KR%d" % c, "use%d" % c, "bL", False, k == 0)
+
+        def zs():
+            act(T.MB[:], T.W37[:].indirect(ML[:]), F.Copy, "W37 " + mr, "MB")
+            mm(T.bO[:, 0:B], T.BW[:], Z[:], "BW " + zr, "uR", "bO")
+            mm(T.bO[:, B:2 * B], T.BW[:], Z[:], "BW " + zr, "xR", "bO", True, False)
+            mm(T.bO[:, B:2 * B], T.IDN[:], T.MB[:], "IDN MB", "xR", "bO", False, True)
+            mm(T.bF[:, 0:B], T.IDN[:], Z[:], "IDN " + zr, "d16", "bF", True, False)
+            mm(T.bF[:, 0:B], T.NID[:], T.GB[:], "NID GB0 GB1", "d16", "bF", False, True)
+            for r in range(16):
+                mm(L(0), slot(T.WE, r), Z[:, r::16], "WE " + zr, "uL", "bL", r == 0, r == 15)
+
+        def c16():
+            act(T.C16[:], T.bF[:, 0:B], F.Sign, "d16 half", "C16", "bF", bias=cf(21))
+            for r in range(16):
+                mm(L(16), slot(T.E0, r), T.C16[:, r::16], "E0 C16", "gL", "bL", r == 0, r == 15)
+            for h in range(2):
+                mm(T.bL[:, 32 + 8 * h:40 + 8 * h], T.C16[:, 128 * h:128 * h + 128], T.E0[:, 15:128:16], "E0 C16", "gT%d" % h, "bL")
+            mm(T.bF[:, B:2 * B], T.BO[:], T.C16[:], "BO C16", "gR", "bF")
+
+        def pairs(i):
+            bn = "bG%d" % (i & 1)
+            bg = T[bn]
+            if i < 4:
+                for h in range(2):
+                    mm(bg[:, :, 16 * h:16 * h + 16], T["BLO" if h else "BLE"][32 * i:32 * i + 32, 0:128], T.BR[32 * i:32 * i + 32, :], "BLE BLO BR", bn, bn)
+                act(T.EQ0[:, :, 32 * i:32 * i + 32], bg[:], F.Relu, bn + " bias0", "EQ0%d" % i, bn, bias=cf(19), scale=512.0)
+                return
+            two = (2 * (i - 4), 2 * (i - 4) + 1)
+            for q, a in enumerate(two):
+                if q:
+                    need("T", [("T", cnt["T"])])
+                for h in range(2):
+                    mm(bg[:, 8 * q:8 * q + 8, 16 * h:16 * h + 16], T["BLO" if h else "BLE"][32 * a:32 * a + 32, 128:256],
+                       T.BR[32 * a:32 * a + 32, 128:256], "BLE BLO BR", bn, bn)
+            for q, a in enumerate(two):
+                act(T.EQ1[:, :, 32 * a:32 * a + 32], bg[:, 8 * q:8 * q + 8, :], F.Relu, bn + " bias1", "EQ1%d" % a, bn, bias=cf(20), scale=512.0)
+
+        def ok(h):
+            s0, s1 = HALF[h]
+            ts(T.OK[:, s0:s1], T.bM[:, s0:s1], thdc, None, A.is_ge, None, "met%d %s" % (h, thd), "OK%d" % h, "bM")
+
+        def oh(h):
+            s0, s1 = HALF[h]
+            mm(T.bF[:, s0:s1], T.UP[:], T.OK[:, s0:s1], "UP OK%d C16" % h, "first%d" % h, "bF", True, False)
+            mm(T.bF[:, s0:s1], T.NEG[:], T.GREP[:, s0:s1], "NEG GREP", "first%d" % h, "bF", False, True)
+            ts(T.OH[:, s0:s1], T.bF[:, s0:s1], 1.0, None, A.is_ge, None, "first%d" % h, "OH%d" % h, "bF")
+
+        def vl(h):
+            s0, s1 = HALF[h]
+            o = T.bL[:, 64 + 8 * h:72 + 8 * h]
+            mm(o, T.IDN[:], T.B32[:], "IDN B32", "vl%d" % h, "bL", True, False)
+            for r in range(16):
+                mm(o, slot(T.WJ, r), T.OH[:, s0 + r:s1:16], "WJ OH%d" % h, "vl%d" % h, "bL", False, r == 15)
+            mm(T.bF[:, B + s0:B + s1], T.DT[:, 128 * t:128 * t + 128], T.OH[:, s0:s1], "DT OH%d GREP" % h, "de%d" % h, "bF")
+
+        def dl(h):
+            o = T.bL[:, 64 + 8 * h:72 + 8 * h]
+            tt(lh(1, h), o, T.SL[:, 0:8], A.not_equal, "vl%d b32f" % h, "any%d" % h, "bL")
+            ts(T.AOFF[:, 8 * h:8 * h + 8], o, 2.0, None, A.add, None, "vl%d" % h, "AOFF%d" % h, "bL")
+            tt(lh(2, h), lh(1, h), lh(0, h), A.mult, "any%d dm" % h, "mmx%d" % h)
+            tt(lh(3, h), lh(2, h), T.LI[:, 48 + 8 * h:56 + 8 * h], A.add, "mmx%d to" % h, "mn%d" % h)
+
+        def sm(h):
+            if not last:
+                c0, c1 = 8 * h, 8 * h + 8
+                tc(T["MO%d" % (t + 1)][:, c0:c1], lh(3, h), "mn%d" % h, "MO%d" % h)
+                send("ML", t + 1, h, c0, c1, T["MO%d" % (t + 1)], "MO%d" % h)
+            elif h:
+                dma("Y", T.ym[:], lf(3), "o_ym", "mn0 mn1", "")
+
+        def t1(h):
+            s0, s1 = HALF[h]
+            tt(T.T1[:, s0:s1], T.D0[:, 32 * s0:32 * s1].indirect(T.AOFF[:, 8 * h:8 * h + 8]), Z[:, s0:s1], A.subtract,
+               "AOFF%d d0a%d d0z%d %s" % (h, h, h, zh[h]), "T1%d" % h)
+
+        def t2(h):
+            s0, s1 = HALF[h]
+            act(T.T2[:, s0:s1], T.T1[:, s0:s1], F.Relu, "T1%d c255" % h, "T2%d" % h, bias=cf(22))
+
+        def t3(h):
+            s0, s1 = HALF[h]
+            tt(T.T3[:, s0:s1], T.T2[:, s0:s1], T.bF[:, B + s0:B + s1], A.add, "T2%d de%d" % (h, h), "T3%d" % h, "bF")
+
+        def sz(h):
+            s0, s1 = HALF[h]
+            out = T.ZF if last else T["ZO%d" % (t + 1)]
+            act(out[:, s0:s1], T.T3[:, s0:s1], F.Abs, "T3%d cm255" % h, "ZO%d" % h, bias=cf(23))
+            if last:
+                dma("Y", T.yz[:, s0:s1], out[:, s0:s1], "o_yz%d" % h, "ZO%d" % h, "")
+            else:
+                send("Z", t + 1, h, s0, s1, out, "ZO%d" % h)
+
+        def conf():
+            e0 = " ".join("EQ0%d" % a for a in range(4))
+            e1 = " ".join("EQ1%d" % a for a in range(4))
+            for c in range(16):
+                o = T.bL[:, 128 + 8 * c:136 + 8 * c]
+                mm(o, T.EQ0[:, c, :], T.GLT[:, 16:24], "GLT " + e0, "CT", "bL", True, c < 8)
+                if c >= 8:
+                    mm(o, T.EQ1[:, c - 8, :], T.GLT[:, 24:32], "GLT " + e1, "CT", "bL", False, True)
+
+        def asum():
+            if not last:
+                for j in range(16):
+                    mm(T.bL[:, 80:81], T.ONE[:], T.GLT[:, j:j + 1], "ONE GLT", "as0", "bL", j == 0, j == 15)
+
+        def par():
+            if not last:
+                tc(T.AI[:, 0:1], T.bL[:, 80:81], "as0", "as2", "bL")
+                ts(T.AI[:, 1:2], T.AI[:, 0:1], 1, None, A.bitwise_and, None, "as2", "as3")
+                ts(T.THR[:, t + 1:t + 2], T.AI[:, 1:2], 2.0, float(2 * QU - 16), A.mult, A.add, "as3", "thd%d" % (t + 1))
+                ts(T.THR[:, t + 5:t + 6], T.AI[:, 1:2], -2.0, 17.0 - 2 * QU, A.mult, A.add, "as3", "thb%d" % (t + 1))
+
+        def cx():
+            op("V", lambda: V.tensor_tensor_scan(T.CX[:], T.DX[:], T.bL[:, 128:256], 0.0, A.add, A.max), "DX CT", "CX", "bL")
+            ts(lf(6), T.CX[:, 7::8], cf(18), None, A.is_le, None, "CX nb", "free")
+            tt(lf(7), lf(6), lf(5), A.mult, "free gd", "w2")
+            tt(lf(8), lf(7), T.SL[:, 16:32], A.add, "w2 b512", "off")
+            tc(T.OFF[:], lf(8), "off", "OFF")
+
+        def ml():
+            tc(li(0), ML[:], mr, "mI")
+            ts(li(1), li(0), 37.0, None, A.mult, None, "mI", "m37")
+            if t == 0:
+                later_const()
+
+        def toL():
+            tt(li(2), L(0), li(1), A.add, "uL m37", "to0", "bL")
+            ts(li(3), li(2), M - 1, None, A.bitwise_and, None, "to0", "to")
+            tt(lf(0), li(0), li(3), A.subtract, "mI to", "dm")
+
+        def td():
+            tt(lf(4), li(3), T.SL[:, 16:32], A.subtract, "to b512", "td")
+            tt(lf(5), lf(4), T.GLT[:, 0:16], A.mult, "td GLT", "gd")
+
+        def oP():
+            act(T.bO[:, 0:B], T.OF[:], F.Copy, "OF UI", "oP", "bO")
+            act(T.bO[:, B:2 * B], T.OF[:], F.Identity, "OF XQ c1184", "oK", "bO", bias=cf(16), scale=32.0)
+
+        one = {
+            "of": lambda: tc(T.OF[:], T.O16[:], "O160 O161", "OF"),
+            "ui": lambda: tc(T.UI[:], T.bO[:, 0:B], "uR", "UI", "bO"),
+            "uu": lambda: ts(T.UU[:], T.UI[:], W - 1, None, A.bitwise_and, None, "UI", "UU"),
+            "xq": lambda: ts(T.XQ[:], T.bO[:, B:2 * B], cf(15), cf(5), A.mult, A.add, "xR cb cb2", "XQ", "bO"),
+            "bit": lambda: ts(T.BIT[:], T.XQ[:], 1, None, A.bitwise_and, None, "XQ", "BIT"),
+            "br": lambda: tt(T.BR[:], T.BIT[:], T.bM[:, B:2 * B], A.add, "BIT CONST", "BR", "bM"),
+            "ble": lambda: ts(T.BLE[:], T.BIT[:], cf(8), cf(9), A.mult, A.add, "BIT e1 e2", "BLE"),
+            "blo": lambda: ts(T.BLO[:], T.BIT[:], cf(10), cf(11), A.mult, A.add, "BIT o1 o2", "BLO"),
+            "glt": lambda: ts(T.GLT[:], T.bL[:, 16:48], thdc, None, A.is_ge, None, "gL gT0 gT1 " + thd, "GLT", "bL"),
+            "grep": lambda: act(T.GREP[:], T.bF[:, B:2 * B], F.Sign, "gR thb%d" % t, "GREP", "bF", bias=T.THR[:, 4 + t:5 + t]),
+            "fq": lambda: tt(T.FQ[:], T.bO[:, 0:B], T.UU[:], A.mult, "oP UU", "FQ", "bO"),
+            "ft": lambda: tt(T.FT[:], T.FQ[:], T.bO[:, B:2 * B], A.add, "FQ oK", "FT", "bO"),
+            "fr": lambda: ts(T.FR[:], T.FT[:], 5, W - 1, A.arith_shift_right, A.bitwise_and, "FT", "FR"),
+            "df": lambda: tt(T.DF[:], T.FR[:], T.bO[:, 0:B], A.subtract, "FR oP", "DF", "bO"),
+            "low": lambda: ts(T.bO[:, B:2 * B], T.bL[:, B:2 * B], float(TH), None, A.is_lt, None, "use0 use1", "oK", "bL bO"),
+            "ldf": lambda: tt(T.LDF[:], T.bO[:, B:2 * B], T.DF[:], A.mult, "oK DF", "LDF", "bO"),
+            "wr": lambda: tt(T.MC[:, 0:M + B].indirect(T.OFF[:]), T.LDF[:], T.OF[:], A.add, "LDF OF OFF", "MC"),
+            "ml": ml, "zs": zs, "c16": c16, "toL": toL, "oP": oP, "conf": conf, "td": td, "cx": cx, "as": asum, "par": par, "fl": flush}
+        per = {"o16": o16, "GB": GB, "ad": ad, "prs": prs, "prv": prv_, "gw": gw, "scan": scan, "use": use, "ok": ok, "oh": oh, "vl": vl, "dl": dl,
+               "sm": sm, "t1": t1, "t2": t2, "t3": t3, "sz": sz}
+
+        def run(x):
+            a, _, b = x.partition(":")
+            if a in per:
+                per[a](int(b))
+            elif b:
+                diff(int(a[1:]), int(b))
+            elif a in one:
+                one[a]()
+            else:
+                pairs(int(a[1:]))
+            if t == 0 and x == "grep":
+                passes()
+        return run
+
+    runs = [step(t) for t in range(T_STEPS)]
+    for x in ORDER:
+        if x[0] == "+":
+            runs[0](x[1:])
+    for t in range(T_STEPS):
+        for x in ORDER:
+            if x[0] != "+":
+                runs[t](x)
+            elif t + 1 < T_STEPS:
+                runs[t + 1](x[1:])
+    dma("Y", T.ymc[:], T.MC[:, 0:M], "o_ymc", "MC", "")
+    need("G", [(s, cnt[s]) for s in ("V", "S", "T", "G")])
+    need("G", [("l_" + x, 16) for x in LOADS] + [("o_" + x, 16) for x in OUTS])
+    for t in range(1, T_STEPS):
+        for h in range(2):
+            for b in "mz":
+                need("G", [("r%s%d%d" % (b, t, h), len(eng(prv, core))), ("s%s%d%d" % (b, t, h), len(eng(core, nxt)))])

@@ -5,11 +5,11 @@ F = ActivationFunctionType
 T_STEPS, W, M, B, QU, TH = 4, 2048, 512, 256, 12, 254
 BIG = 131072.0
 HALF = [(0, 128), (128, 256)]
-VPR = [16, 0]
-CMPV = ["VVVV", "VSSS"]
-ORDER = ("GB:0 prs:0 o16:1 ml prv:0 GB:1 zs gw:0 c16 prs:1 scan:0 grep xq bit ble blo br use:0 toL d0:3 d0:2 glt of ad:1 prv:1 d0:1 d0:0 ui fl "
-         "ok:0 gw:1 oh:0 p0 p1 vl:0 scan:1 p2 dl:0 t1:0 p3 oP p4 p5 t2:0 use:1 sm:0 uu td conf fq ft d1:3 t3:0 sz:0 fr d1:2 low df ldf cx wr "
-         "+o16:0 d1:1 +ad:0 d1:0 fl ok:1 oh:1 vl:1 dl:1 t1:1 as t2:1 sm:1 t3:1 par sz:1").split()
+VPR = [32, 16]
+CMPV = ["VVVS", "SSSS"]
+ORDER = ("ml o16:1 prs:0 GB:1 zs c16 prs:1 prv:0 gw:0 scan:0 prv:1 xq of bit br ble use:0 grep ui d0:3 toL d0:2 glt d0:1 d0:0 ad:1 blo fl "
+         "ok:0 p0 gw:1 oh:0 p1 scan:1 vl:0 p2 dl:0 p3 p4 sm:0 oP p5 uu fq d1:3 ft fr td t1:0 df use:1 conf t2:0 low ldf cx d1:2 t3:0 wr "
+         "d1:1 d1:0 fl +o16:0 ok:1 oh:1 vl:1 dl:1 sz:0 sm:1 +ad:0 t1:1 as t2:1 par t3:1 +GB:0 sz:1").split()
 SB, PS = "sbuf", "psum"
 BF, F4, I4, U2 = "bfloat16", "float32", "int32", "uint16"
 SCRATCH = {"CMP": (SB, [128, B, 16], BF), "EQ0": (SB, [128, 16, 128], BF), "EQ1": (SB, [128, 8, 128], BF),
@@ -176,6 +176,30 @@ def rank_program(g, core, T, topo):
     ts(cf(12), cf(6), 2.0 ** -9, None, A.mult, None, "is9", "c9")
     ts(cf(13), cf(5), -0.5, None, A.mult, None, "le8", "nle8")
     tt(T.TB[:, 0:16], T.TB[:, 32:48], T.TB[:, 48:64], A.mult, "tbc tbm", "tba")
+
+    def zeros(c):
+        lo, hi = 32 * HALF[c][0], 32 * HALF[c][1]
+        ms(T.D0[:, lo:hi:2], 0.0, "d0z%d" % c)
+        ms(T.D0[:, lo:hi:32], -512.0, "d0z%d" % c)
+        if c:
+            ms(T.D1[:, lo + 1:hi:2], 0.0, "d1z%d" % c)
+        else:
+            act(T.D1[:, lo + 1:hi:2], T.D0[:, lo:hi:2], F.Copy, "d0z0", "d1z0", scale=0.0)
+
+    zeros(0)
+    ms(cf(21), 0.5, "half")
+    ms(cf(22), 255.0, "c255")
+    ms(cf(23), -255.0, "cm255")
+    ms(T.THR[:, 0:1], float(2 * QU - 16), "thd0")
+    ms(T.THR[:, 4:5], 17.0 - 2 * QU, "thb0")
+    op("V", lambda: V.tensor_reduce(cf(14), T.TB[:, 0:16], AxisListType.X, A.add), "tba", "cb0")
+    ts(cf(8), cf(5), cf(4), None, A.mult, None, "le8 even", "e1")
+    ts(cf(9), cf(7), cf(4), None, A.mult, None, "base even", "e2")
+    ts(cf(10), cf(5), cf(2), None, A.mult, None, "le8 odd", "o1")
+    ts(cf(11), cf(7), cf(2), None, A.mult, None, "base odd", "o2")
+    ts(cf(15), cf(14), cf(5), None, A.mult, None, "cb0 le8", "cb")
+    ts(cf(5), cf(14), 0.5, -0.5, A.mult, A.add, "cb0 cb", "cb2 le8")
+    ts(cf(17), cf(0), 2.0, -1.0, A.mult, A.add, "kf", "cj")
     tc(T.ML0[:], T.M0[:], "M0", "ML0_0 ML0_1")
     ms(T.MC[:, M:M + B], 0.0, "MC")
     tc(T.MC[:, 0:M], T.MCI[:], "MCI", "MC")
@@ -185,22 +209,9 @@ def rank_program(g, core, T, topo):
         ts(T.BW[:], T.BO[:], T.WT[:, 0:1], None, A.mult, None, "BO WT", "BW")
         ts(T.WE[:], T.E0[:], T.WT[:, 0:1], None, A.mult, None, "E0 WT", "WE")
         ts(T.WJI[:], T.WI[:], M - 1, None, A.bitwise_and, None, "WI", "WJI")
-        ms(cf(21), 0.5, "half")
-        ms(cf(22), 255.0, "c255")
-        ms(cf(23), -255.0, "cm255")
-        ms(T.THR[:, 0:1], float(2 * QU - 16), "thd0")
-        ms(T.THR[:, 4:5], 17.0 - 2 * QU, "thb0")
         ts(T.W37[:], T.WJI[:], -256.0, None, A.add, None, "WJI", "W37")
-        op("V", lambda: V.tensor_reduce(cf(14), T.TB[:, 0:16], AxisListType.X, A.add), "tba", "cb0")
-        ts(cf(8), cf(5), cf(4), None, A.mult, None, "le8 even", "e1")
-        ts(cf(9), cf(7), cf(4), None, A.mult, None, "base even", "e2")
-        ts(cf(10), cf(5), cf(2), None, A.mult, None, "le8 odd", "o1")
-        ts(cf(11), cf(7), cf(2), None, A.mult, None, "base odd", "o2")
         ts(T.bM[:, B:2 * B], T.IOT[:], cf(12), cf(13), A.mult, A.add, "IOT c9 nle8", "CONST", "bM")
-        ts(cf(15), cf(14), cf(5), None, A.mult, None, "cb0 le8", "cb")
-        ts(cf(5), cf(14), 0.5, -0.5, A.mult, A.add, "cb0 cb", "cb2 le8")
         ts(cf(16), cf(0), 1184.0, None, A.mult, None, "kf", "c1184")
-        ts(cf(17), cf(0), 2.0, -1.0, A.mult, A.add, "kf", "cj")
         ts(cf(18), cf(1), -BIG, 7 * BIG + 0.5, A.mult, A.add, "gf", "nb")
         ts(cf(19), cf(3), -1.0, -1152.0, A.mult, A.add, "pf", "bias0")
         ts(cf(20), cf(3), -1.0, -1280.0, A.mult, A.add, "pf", "bias1")
@@ -218,12 +229,6 @@ def rank_program(g, core, T, topo):
         aff(T.UP, T.U1, [[-1, 128]], A.is_ge, 0.0, 0, 1, "U1", "UP")
         aff(T.DX2, T.DX1, [[0, 16], [-16, 8]], A.is_ge, BIG, 0, 1, "DX1", "DX2")
         aff(T.DX, T.DX2, [[0, 16], [16, 8]], A.is_ge, BIG, 15, -1, "DX2", "DX")
-
-    def zeros(c):
-        s0, s1 = HALF[c]
-        ms(T.D0[:, 32 * s0:32 * s1:2], 0.0, "d0z%d" % c)
-        ms(T.D0[:, 32 * s0:32 * s1:32], -512.0, "d0z%d" % c)
-        ms(T.D1[:, 32 * s0 + 1:32 * s1:2], 0.0, "d1z%d" % c)
 
     def passes():
         for t in range(T_STEPS):
@@ -270,8 +275,6 @@ def rank_program(g, core, T, topo):
 
         def gw(c):
             s0, s1 = HALF[c]
-            if t == 0:
-                zeros(c)
             tc(T.P0[:, s0:s1], T.D1[:, 32 * s0:32 * s1:32], "d1v%d d1s%d" % (c, c), "P0%d" % c)
             tc(T.D1[:, 32 * s0 + 32:32 * s1:32], T.GB[:, s0:s1 - 1], "GB%d" % c, "d1v%d d1s%d" % (c, c))
 
@@ -323,6 +326,8 @@ def rank_program(g, core, T, topo):
                 mm(L(0), slot(T.WE, r), Z[:, r::16], "WE " + zr, "uL", "bL", r == 0, r == 15)
 
         def c16():
+            if t == 0:
+                zeros(1)
             act(T.C16[:], T.bF[:, 0:B], F.Sign, "d16 half", "C16", "bF", bias=cf(21))
             for r in range(16):
                 mm(L(16), slot(T.E0, r), T.C16[:, r::16], "E0 C16", "gL", "bL", r == 0, r == 15)

from concourse.mybir import dt, AluOpType, AxisListType, ActivationFunctionType
A = AluOpType
F = ActivationFunctionType

T_STEPS, W, M, B, QU, TH = 4, 2048, 512, 256, 12, 254
BIG = 131072.0
HALF = [(0, 128), (128, 256)]
VPR = [32, 16]
CMPV = ["VVVS", "SSSS"]
ORDER = ("ml o16:1 prs:0 GB:1 zs c16 prs:1 prv:0 gw:0 scan:0 prv:1 xq of bit br ble use:0 grep ui d0:3 toL d0:2 glt d0:1 d0:0 ad:1 blo fl "
         "ok:0 p0 gw:1 oh:0 p1 scan:1 vl:0 p2 dl:0 p3 p4 sm:0 oP p5 uu fq d1:3 ft fr td t1:0 df use:1 conf t2:0 low ldf cx d1:2 t3:0 wr "
         "d1:1 d1:0 fl +o16:0 ok:1 oh:1 vl:1 dl:1 sz:0 sm:1 +ad:0 t1:1 as t2:1 par t3:1 +GB:0 sz:1").split()
SB, PS = "sbuf", "psum"
BF, F4, I4, U2 = "bfloat16", "float32", "int32", "uint16"
SCRATCH = {"CMP": (SB, [128, B, 16], BF), "EQ0": (SB, [128, 16, 128], BF), "EQ1": (SB, [128, 8, 128], BF),
           "bD0": (PS, [128, 128, 4], F4), "bD1": (PS, [128, 128, 4], F4), "bG0": (PS, [128, 16, 32], F4), "bG1": (PS, [128, 16, 32], F4)}
for _n, _w, _d in ([(x, 512, F4) for x in ("bM", "bL", "bF", "bO")]
                   + [("PRW", W, BF), ("ADW", W, BF), ("GLW", M, BF), ("MCI", M, I4), ("MC", M + B, F4), ("WI", M, I4), ("WJI", M, I4), ("W37", M, BF),
                      ("M0", 16, I4), ("DV", 4, BF), ("WT", 1, BF), ("O16", B, U2), ("D0", 32 * B, BF), ("D1", 32 * B, BF), ("KR", 32 * B, BF),
                      ("AOFF", 16, U2), ("OFF", 16, U2), ("GLT", 32, BF), ("CX", 128, F4), ("LI", 64, I4), ("LF", 144, F4), ("CI", 4, I4),
                      ("CF", 24, F4), ("THR", 8, F4), ("AI", 2, I4), ("DG", 512, BF), ("DT", 512, BF), ("IOT", B, F4), ("TB", 64, F4), ("SL", 48, F4), ("B32", 8, BF)]
                   + [(x, 144, BF) for x in ("E1", "E2", "E0", "EH", "NE", "WE", "WJ")]
                   + [(x, B, BF) for x in ("GB", "MB", "C16", "P0", "BLE", "BLO", "BR", "GREP", "OK", "OH")]
                   + [(x, B, I4) for x in ("UI", "UU", "FQ", "FT", "FR", "XQ", "BIT")]
                   + [(x, B, F4) for x in ("OF", "DF", "LDF", "T1", "T2", "T3", "ZF")]
                   + [(x, 128, F4) for x in ("DX1", "DX2", "DX")]
                   + [(x, 128, BF) for x in ("ONE", "BO1", "BO", "IDN", "NID", "NBO", "U1", "UP", "NEG", "BW")]):
    SCRATCH[_n] = (PS if _n in ("bM", "bL", "bF", "bO") else SB, [128, _w], _d)
LOADS = ["m0", "mc", "z0", "gl", "wt", "dv", "pr", "ad"]
OUTS = ["ymc", "yz0", "yz1", "ym"]
SEMAPHORES = ["V", "S", "T", "G"] + ["l_" + n for n in LOADS] + ["o_" + n for n in OUTS]
for _t in range(T_STEPS):
    SCRATCH["Z%d" % _t] = (SB, [128, B], BF)
    SCRATCH["ML%d" % _t] = (SB, [128, 16], U2)
    if _t:
        SCRATCH["ZO%d" % _t] = (SB, [128, B], BF)
        SCRATCH["MO%d" % _t] = (SB, [128, 16], U2)
        SEMAPHORES += ["%s%s%d%d" % (a, b, _t, h) for a in "rs" for b in "mz" for h in (0, 1)]


def rank_program(g, core, T, topo):
    rank = T.rank_of(core)
    if rank is None:
        return
    n = len(T.cores)
    nxt, prv = T.cores[(rank + 1) % n], T.cores[(rank - 1) % n]
    V, S, P = g.vector, g.scalar, g.tensor
    QS = {"V": V, "S": S, "T": P, "G": g, "Y": g.sync}
    cnt = {e: 0 for e in QS}
    clock = {e: {} for e in QS}
    snap = {}
    wrote, read, bank = {}, {}, {}

    def need(e, pairs):
        want = {}
        for s, v in pairs:
            want[s] = max(want.get(s, 0), v)
        for s, v in want.items():
            if clock[e].get(s, 0) < v:
                QS[e].wait_ge(T.sem[s], v)
                clock[e][s] = v
                for s2, v2 in snap.get((s, v), {}).items():
                    clock[e][s2] = max(clock[e].get(s2, 0), v2)

    def deps(e, r, w, b):
        p = [wrote[x] for x in r]
        for x in w:
            q = ([wrote[x]] if x in wrote else []) + list(read.get(x, {}).items())
            p += [y for y in q if not (e == "T" and y[0] == "T")]
        for x in b:
            p += [q for q in bank.get(x, {}).items() if q[0] != e]
        need(e, p)

    def mark(tag, r, w, b):
        for x in r:
            d = read.setdefault(x, {})
            d[tag[0]] = max(d.get(tag[0], 0), tag[1])
        for x in w:
            wrote[x] = tag
            read[x] = {}
        for x in b:
            bank.setdefault(x, {})[tag[0]] = tag[1]

    def op(e, fn, r="", w="", b=""):
        r, w, b = r.split(), w.split(), b.split()
        deps(e, r, w, b)
        cnt[e] += 1
        fn().then_inc(T.sem[e], 1)
        snap[(e, cnt[e])] = dict(clock[e])
        mark((e, cnt[e]), r, w, b)

    def dma(e, out, in_, sem, r="", w=""):
        r, w = r.split(), w.split()
        deps(e, r, w, [])
        QS[e].dma_start(out, in_).then_inc(T.sem[sem], 16)
        mark((sem, 16), r, w, [])

    eng = lambda a, b: topo.engines(a, b)[:8]

    def send(buf, t, h, c0, c1, src, r):
        rid, pid = topo.addr(nxt, core)
        deps("G", [r], [], [])
        k = ("m" if buf == "ML" else "z") + "%d%d" % (t, h)
        g.remote_dma(T[buf + str(t)][:, c0:c1], src[:, c0:c1], T.sem["r" + k], T.sem["s" + k], pid, rid, sum(1 << e for e in eng(core, nxt)))
        mark(("s" + k, len(eng(core, nxt))), [r], [], [])
        wrote["%s%d_%d" % (buf, t, h)] = ("r" + k, len(eng(prv, core)))

    def mm(out, l, rr, r, w, b, st=True, sp=True):
        op("T", lambda: P.matmul(out, l, rr, st, sp), r, w, b)

    def tt(out, a, c, o, r, w, b=""):
        op("V", lambda: V.tensor_tensor(out, a, c, o), r, w, b)

    def ts(out, a, s1, s2, o1, o2, r, w, b=""):
        if o2 is None:
            op("V", lambda: V.tensor_scalar(out, a, s1, None, o1), r, w, b)
        else:
            op("V", lambda: V.tensor_scalar(out, a, s1, s2, o1, o2), r, w, b)

    def tc(out, a, r, w, b=""):
        op("V", lambda: V.tensor_copy(out, a), r, w, b)

    def ms(out, c, w):
        op("V", lambda: V.memset(out, c), "", w)

    def act(out, a, f, r, w, b="", **kw):
        op("S", lambda: S.activation(out, a, f, **kw), r, w, b)

    def aff(o, i, pat, cmp, fill, base, cm, r, w):
        op("G", lambda: g.affine_select(o[:], i[:], pat, cmp, fill, base, cm), r, w)

    def slot(pad, k):
        return pad[:, 15 - k:143 - k]

    cf = lambda i: T.CF[:, i:i + 1]
    li = lambda i: T.LI[:, 16 * i:16 * i + 16]
    lf = lambda i: T.LF[:, 16 * i:16 * i + 16]
    lh = lambda i, h: T.LF[:, 16 * i + 8 * h:16 * i + 8 * h + 8]
    L = lambda i: T.bL[:, i:i + 16]

    dma("Y", T.M0[:], T.m0[:], "l_m0", "", "M0")
    dma("Y", T.MCI[:], T.mc[:], "l_mc", "", "MCI")
    dma("S", T.GLW[:], T.gl[:], "l_gl", "", "GLW")
    dma("S", T.ADW[:], T.ad[:], "l_ad", "", "ADW")
    dma("Y", T.PRW[:], T.pr[:], "l_pr", "", "PRW")
    dma("Y", T.Z0[:], T.z0[:], "l_z0", "", "Z0_0 Z0_1")
    dma("Y", T.WT[:], T.wt[:], "l_wt", "", "WT")
    dma("Y", T.DV[:], T.dv[:], "l_dv", "", "DV")

    ms(T.ONE[:], 1.0, "ONE")
    ms(T.E1[:], 0.0, "E1")
    ms(T.E1[:, 15::16], 1.0, "E1")
    op("G", lambda: g.iota(T.CI[:, 0:1], [[0, 1]], 0, 1), "", "pc")
    op("G", lambda: g.iota(T.IOT[:], [[1, B]], 0, 0, allow_small_or_imprecise_dtypes=True), "", "IOT")
    aff(T.E2, T.E1, [[-16, 9], [0, 16]], A.is_ge, 0.0, 0, 1, "E1", "E2")
    aff(T.E0, T.E2, [[16, 9], [0, 16]], A.is_ge, 0.0, 15, -1, "E2", "E0")
    aff(T.BO1, T.ONE, [[-16, 8], [0, 16]], A.is_ge, 0.0, 0, 1, "ONE", "BO1")
    aff(T.BO, T.BO1, [[16, 8], [0, 16]], A.is_ge, 0.0, 15, -1, "BO1", "BO")
    aff(T.IDN, T.ONE, [[-1, 128]], A.is_equal, 0.0, 0, 1, "ONE", "IDN")
    op("G", lambda: g.iota(T.WI[:], [[37, M]], 0, 0), "", "WI")
    ts(T.CI[:, 1:2], T.CI[:, 0:1], 15, None, A.bitwise_and, None, "pc", "kc")
    ts(T.CI[:, 2:3], T.CI[:, 0:1], 4, None, A.arith_shift_right, None, "pc", "gc")
    ts(T.CI[:, 3:4], T.CI[:, 0:1], 4, 1, A.arith_shift_right, A.bitwise_and, "pc", "oc")
    ms(T.TB[:, 0:16], 0.5, "tba")
    ms(T.TB[:, 16:32], 0.0, "tbb")
    tc(cf(0), T.CI[:, 1:2], "kc", "kf")
    tc(cf(1), T.CI[:, 2:3], "gc", "gf")
    tc(cf(2), T.CI[:, 3:4], "oc", "odd")
    tc(cf(3), T.CI[:, 0:1], "pc", "pf")
    op("V", lambda: V.tensor_tensor_scan(T.TB[:, 32:48], T.TB[:, 0:16], T.TB[:, 16:32], 2.0, A.mult, A.add), "tba tbb", "tbc")
    ts(cf(5), cf(0), 8.5, None, A.is_le, None, "kf", "le8")
    ts(cf(6), cf(0), 9.0, None, A.is_equal, None, "kf", "is9")
    ts(T.TB[:, 48:64], T.IOT[:, 0:16], cf(0), None, A.is_equal, None, "IOT kf", "tbm")
    ts(cf(4), cf(2), -1.0, 1.0, A.mult, A.add, "odd", "even")
    ts(cf(7), cf(5), -0.5, cf(6), A.mult, A.add, "le8 is9", "base")
    ts(cf(12), cf(6), 2.0 ** -9, None, A.mult, None, "is9", "c9")
    ts(cf(13), cf(5), -0.5, None, A.mult, None, "le8", "nle8")
    tt(T.TB[:, 0:16], T.TB[:, 32:48], T.TB[:, 48:64], A.mult, "tbc tbm", "tba")

    def zeros(c):
        lo, hi = 32 * HALF[c][0], 32 * HALF[c][1]
        ms(T.D0[:, lo:hi:2], 0.0, "d0z%d" % c)
        ms(T.D0[:, lo:hi:32], -512.0, "d0z%d" % c)
        if c:
            ms(T.D1[:, lo + 1:hi:2], 0.0, "d1z%d" % c)
        else:
            act(T.D1[:, lo + 1:hi:2], T.D0[:, lo:hi:2], F.Copy, "d0z0", "d1z0", scale=0.0)

    zeros(0)
    ms(cf(21), 0.5, "half")
    ms(cf(22), 255.0, "c255")
    ms(cf(23), -255.0, "cm255")
    ms(T.THR[:, 0:1], float(2 * QU - 16), "thd0")
    ms(T.THR[:, 4:5], 17.0 - 2 * QU, "thb0")
    op("V", lambda: V.tensor_reduce(cf(14), T.TB[:, 0:16], AxisListType.X, A.add), "tba", "cb0")
    ts(cf(8), cf(5), cf(4), None, A.mult, None, "le8 even", "e1")
    ts(cf(9), cf(7), cf(4), None, A.mult, None, "base even", "e2")
    ts(cf(10), cf(5), cf(2), None, A.mult, None, "le8 odd", "o1")
    ts(cf(11), cf(7), cf(2), None, A.mult, None, "base odd", "o2")
    ts(cf(15), cf(14), cf(5), None, A.mult, None, "cb0 le8", "cb")
    ts(cf(5), cf(14), 0.5, -0.5, A.mult, A.add, "cb0 cb", "cb2 le8")
    ts(cf(17), cf(0), 2.0, -1.0, A.mult, A.add, "kf", "cj")
    tc(T.ML0[:], T.M0[:], "M0", "ML0_0 ML0_1")
    ms(T.MC[:, M:M + B], 0.0, "MC")
    tc(T.MC[:, 0:M], T.MCI[:], "MCI", "MC")

    def later_const():
        ts(T.NID[:], T.IDN[:], -1.0, None, A.mult, None, "IDN", "NID")
        ts(T.BW[:], T.BO[:], T.WT[:, 0:1], None, A.mult, None, "BO WT", "BW")
        ts(T.WE[:], T.E0[:], T.WT[:, 0:1], None, A.mult, None, "E0 WT", "WE")
        ts(T.WJI[:], T.WI[:], M - 1, None, A.bitwise_and, None, "WI", "WJI")
        ts(T.W37[:], T.WJI[:], -256.0, None, A.add, None, "WJI", "W37")
        ts(T.bM[:, B:2 * B], T.IOT[:], cf(12), cf(13), A.mult, A.add, "IOT c9 nle8", "CONST", "bM")
        ts(cf(16), cf(0), 1184.0, None, A.mult, None, "kf", "c1184")
        ts(cf(18), cf(1), -BIG, 7 * BIG + 0.5, A.mult, A.add, "gf", "nb")
        ts(cf(19), cf(3), -1.0, -1152.0, A.mult, A.add, "pf", "bias0")
        ts(cf(20), cf(3), -1.0, -1280.0, A.mult, A.add, "pf", "bias1")
        ts(T.SL[:, 32:48], T.IOT[:, 0:16], 16.0, cf(0), A.mult, A.add, "IOT kf", "sl")
        ms(T.DX1[:], -16.0 * BIG, "DX1")
        ts(T.NBO[:], T.BO[:], -1.0, None, A.mult, None, "BO", "NBO")
        ts(T.NEG[:], T.BO[:], -0.03125, None, A.mult, None, "BO", "NEG")
        ts(T.NE[:], T.E0[:], -1.0, None, A.mult, None, "E0", "NE")
        ts(T.EH[:], T.E0[:], 2.0, None, A.mult, None, "E0", "EH")
        ts(T.WJ[:], T.E0[:], cf(17), None, A.mult, None, "E0 cj", "WJ")
        ts(T.SL[:, 0:16], T.SL[:, 32:48], 32.0, None, A.mult, None, "sl", "b32f")
        ts(T.SL[:, 16:32], T.SL[:, 32:48], float(M), None, A.add, None, "sl", "b512")
        tc(T.B32[:], T.SL[:, 0:8], "b32f", "B32")
        aff(T.U1, T.NBO, [[-1, 128]], A.not_equal, 1.0, 0, 1, "NBO", "U1")
        aff(T.UP, T.U1, [[-1, 128]], A.is_ge, 0.0, 0, 1, "U1", "UP")
        aff(T.DX2, T.DX1, [[0, 16], [-16, 8]], A.is_ge, BIG, 0, 1, "DX1", "DX2")
        aff(T.DX, T.DX2, [[0, 16], [16, 8]], A.is_ge, BIG, 15, -1, "DX2", "DX")

    def passes():
        for t in range(T_STEPS):
            ts(T.DG[:, 128 * t:128 * t + 128], T.IDN[:], T.DV[:, t:t + 1], None, A.mult, None, "IDN DV", "DG%d" % t)
        mm(T.bF[:], T.BO[:], T.DG[:], "BO DG0 DG1 DG2 DG3", "dtp", "bF")
        tc(T.DT[:], T.bF[:], "dtp", "DT", "bF")

    def step(t):
        last = t == T_STEPS - 1
        Z, ML = T["Z%d" % t], T["ML%d" % t]
        zh, mh = ["Z%d_0" % t, "Z%d_1" % t], ["ML%d_0" % t, "ML%d_1" % t]
        zr, mr, thd = " ".join(zh), " ".join(mh), "thd%d" % t
        thdc = T.THR[:, t:t + 1]
        pend = []
        for x in ("d1v0", "d1v1", "d1s0", "d1s1"):
            wrote.setdefault(x, ("V", 1))

        def kr(c, i):
            return T.KR[:, 32 * HALF[c][0] + i:32 * HALF[c][1]:32]

        def o16(c):
            s0, s1 = HALF[c]
            tc(T.O16[:, s0:s1], T.MC[:, 0:M].indirect(ML[:, 8 * c:8 * c + 8]), "MC " + mh[c], "O16%d" % c)

        def GB(c):
            s0, s1 = HALF[c]
            act(T.GB[:, s0:s1], T.GLW[:].indirect(ML[:, 8 * c:8 * c + 8]), F.Copy, "GLW " + mh[c], "GB%d" % c)

        def ad(c):
            s0, s1 = HALF[c]
            act(T.D0[:, 32 * s0 + 1:32 * s1:2], T.ADW[:].indirect(T.O16[:, s0:s1]), F.Copy, "ADW O16%d" % c, "d0a%d" % c, scale=-1.0)

        def prs(c):
            s0, s1 = HALF[c]
            s0 += VPR[c]
            if s1 > s0:
                act(T.D1[:, 32 * s0:32 * s1:2], T.PRW[:].indirect(T.O16[:, s0:s1]), F.Copy, "PRW O16%d" % c, "d1s%d" % c)

        def prv_(c):
            s0 = HALF[c][0]
            s1 = s0 + VPR[c]
            if s1 > s0:
                tc(T.D1[:, 32 * s0:32 * s1:2], T.PRW[:].indirect(T.O16[:, s0:s1]), "PRW O16%d" % c, "d1v%d" % c)

        def gw(c):
            s0, s1 = HALF[c]
            tc(T.P0[:, s0:s1], T.D1[:, 32 * s0:32 * s1:32], "d1v%d d1s%d" % (c, c), "P0%d" % c)
            tc(T.D1[:, 32 * s0 + 32:32 * s1:32], T.GB[:, s0:s1 - 1], "GB%d" % c, "d1v%d d1s%d" % (c, c))

        def scan(c):
            s0, s1 = HALF[c]
            hi, lo = 32 * s1 - 1, 32 * s0 - 1 if s0 else None
            op("V", lambda: V.tensor_tensor_scan(T.KR[:, hi:lo:-1], T.D0[:, hi:lo:-1], T.D1[:, hi:lo:-1], T.GB[:, s1 - 1:s1], A.add, A.max),
               "GB{0} d0a{0} d0z{0} d1v{0} d1s{0} d1z{0}".format(c), "KR%d" % c)
            tt(kr(c, 0), T.P0[:, s0:s1], kr(c, 1), A.max, "P0%d KR%d" % (c, c), "K0%d" % c)

        def diff(c, q):
            s0, s1 = HALF[c]
            bn = "bD%d" % (q & 1)
            bd = T[bn]
            e = CMPV[c][q]
            for j in range(4):
                mm(bd[:, :, j], T.NID[:], kr(c, 8 * q + 2 * j), "NID KR%d K0%d" % (c, c), bn, bn, True, False)
                mm(bd[:, :, j], T.IDN[:], Z[:, s0:s1], "IDN " + zh[c], bn, bn, False, True)
            name = "cmp%d%d" % (c, q)
            if e == "S":
                act(T.CMP[:, s0:s1, 4 * q:4 * q + 4], bd[:], F.Sign, bn + " half", name, bn, bias=cf(21))
            else:
                ts(T.CMP[:, s0:s1, 4 * q:4 * q + 4], bd[:], 0.0, 0.5, A.is_ge, A.subtract, bn, name, bn)
            flush()
            pend.append((c, q, e, name))

        def flush():
            for c, q, e, name in pend:
                s0, s1 = HALF[c]
                for k in range(4 * q + 3, 4 * q - 1, -1):
                    mm(T.bM[:, s0:s1], slot(T.E0 if e == "S" else T.EH, k), T.CMP[:, s0:s1, k], "E0 EH " + name, "met%d" % c, "bM", k == 15, k == 0)
            del pend[:]

        def use(c):
            s0, s1 = HALF[c]
            for k in range(15, -1, -1):
                up = kr(c, 2 * k + 2) if k < 15 else T.GB[:, s0:s1]
                mm(T.bL[:, B + s0:B + s1], slot(T.E0, k), up, "E0 GB%d KR%d" % (c, c), "use%d" % c, "bL", k == 15, False)
                mm(T.bL[:, B + s0:B + s1], slot(T.NE, k), kr(c, 2 * k + 1), "NE KR%d" % c, "use%d" % c, "bL", False, k == 0)

        def zs():
            act(T.MB[:], T.W37[:].indirect(ML[:]), F.Copy, "W37 " + mr, "MB")
            mm(T.bO[:, 0:B], T.BW[:], Z[:], "BW " + zr, "uR", "bO")
            mm(T.bO[:, B:2 * B], T.BW[:], Z[:], "BW " + zr, "xR", "bO", True, False)
            mm(T.bO[:, B:2 * B], T.IDN[:], T.MB[:], "IDN MB", "xR", "bO", False, True)
            mm(T.bF[:, 0:B], T.IDN[:], Z[:], "IDN " + zr, "d16", "bF", True, False)
            mm(T.bF[:, 0:B], T.NID[:], T.GB[:], "NID GB0 GB1", "d16", "bF", False, True)
            for r in range(16):
                mm(L(0), slot(T.WE, r), Z[:, r::16], "WE " + zr, "uL", "bL", r == 0, r == 15)

        def c16():
            if t == 0:
                zeros(1)
            act(T.C16[:], T.bF[:, 0:B], F.Sign, "d16 half", "C16", "bF", bias=cf(21))
            for r in range(16):
                mm(L(16), slot(T.E0, r), T.C16[:, r::16], "E0 C16", "gL", "bL", r == 0, r == 15)
            for h in range(2):
                mm(T.bL[:, 32 + 8 * h:40 + 8 * h], T.C16[:, 128 * h:128 * h + 128], T.E0[:, 15:128:16], "E0 C16", "gT%d" % h, "bL")
            mm(T.bF[:, B:2 * B], T.BO[:], T.C16[:], "BO C16", "gR", "bF")

        def pairs(i):
            bn = "bG%d" % (i & 1)
            bg = T[bn]
            if i < 4:
                for h in range(2):
                    mm(bg[:, :, 16 * h:16 * h + 16], T["BLO" if h else "BLE"][32 * i:32 * i + 32, 0:128], T.BR[32 * i:32 * i + 32, :], "BLE BLO BR", bn, bn)
                act(T.EQ0[:, :, 32 * i:32 * i + 32], bg[:], F.Relu, bn + " bias0", "EQ0%d" % i, bn, bias=cf(19), scale=512.0)
                return
            two = (2 * (i - 4), 2 * (i - 4) + 1)
            for q, a in enumerate(two):
                if q:
                    need("T", [("T", cnt["T"])])
                for h in range(2):
                    mm(bg[:, 8 * q:8 * q + 8, 16 * h:16 * h + 16], T["BLO" if h else "BLE"][32 * a:32 * a + 32, 128:256],
                       T.BR[32 * a:32 * a + 32, 128:256], "BLE BLO BR", bn, bn)
            for q, a in enumerate(two):
                act(T.EQ1[:, :, 32 * a:32 * a + 32], bg[:, 8 * q:8 * q + 8, :], F.Relu, bn + " bias1", "EQ1%d" % a, bn, bias=cf(20), scale=512.0)

        def ok(h):
            s0, s1 = HALF[h]
            ts(T.OK[:, s0:s1], T.bM[:, s0:s1], thdc, None, A.is_ge, None, "met%d %s" % (h, thd), "OK%d" % h, "bM")

        def oh(h):
            s0, s1 = HALF[h]
            mm(T.bF[:, s0:s1], T.UP[:], T.OK[:, s0:s1], "UP OK%d C16" % h, "first%d" % h, "bF", True, False)
            mm(T.bF[:, s0:s1], T.NEG[:], T.GREP[:, s0:s1], "NEG GREP", "first%d" % h, "bF", False, True)
            ts(T.OH[:, s0:s1], T.bF[:, s0:s1], 1.0, None, A.is_ge, None, "first%d" % h, "OH%d" % h, "bF")

        def vl(h):
            s0, s1 = HALF[h]
            o = T.bL[:, 64 + 8 * h:72 + 8 * h]
            mm(o, T.IDN[:], T.B32[:], "IDN B32", "vl%d" % h, "bL", True, False)
            for r in range(16):
                mm(o, slot(T.WJ, r), T.OH[:, s0 + r:s1:16], "WJ OH%d" % h, "vl%d" % h, "bL", False, r == 15)
            mm(T.bF[:, B + s0:B + s1], T.DT[:, 128 * t:128 * t + 128], T.OH[:, s0:s1], "DT OH%d GREP" % h, "de%d" % h, "bF")

        def dl(h):
            o = T.bL[:, 64 + 8 * h:72 + 8 * h]
            tt(lh(1, h), o, T.SL[:, 0:8], A.not_equal, "vl%d b32f" % h, "any%d" % h, "bL")
            ts(T.AOFF[:, 8 * h:8 * h + 8], o, 2.0, None, A.add, None, "vl%d" % h, "AOFF%d" % h, "bL")
            tt(lh(2, h), lh(1, h), lh(0, h), A.mult, "any%d dm" % h, "mmx%d" % h)
            tt(lh(3, h), lh(2, h), T.LI[:, 48 + 8 * h:56 + 8 * h], A.add, "mmx%d to" % h, "mn%d" % h)

        def sm(h):
            if not last:
                c0, c1 = 8 * h, 8 * h + 8
                tc(T["MO%d" % (t + 1)][:, c0:c1], lh(3, h), "mn%d" % h, "MO%d" % h)
                send("ML", t + 1, h, c0, c1, T["MO%d" % (t + 1)], "MO%d" % h)
            elif h:
                dma("Y", T.ym[:], lf(3), "o_ym", "mn0 mn1", "")

        def t1(h):
            s0, s1 = HALF[h]
            tt(T.T1[:, s0:s1], T.D0[:, 32 * s0:32 * s1].indirect(T.AOFF[:, 8 * h:8 * h + 8]), Z[:, s0:s1], A.subtract,
               "AOFF%d d0a%d d0z%d %s" % (h, h, h, zh[h]), "T1%d" % h)

        def t2(h):
            s0, s1 = HALF[h]
            act(T.T2[:, s0:s1], T.T1[:, s0:s1], F.Relu, "T1%d c255" % h, "T2%d" % h, bias=cf(22))

        def t3(h):
            s0, s1 = HALF[h]
            tt(T.T3[:, s0:s1], T.T2[:, s0:s1], T.bF[:, B + s0:B + s1], A.add, "T2%d de%d" % (h, h), "T3%d" % h, "bF")

        def sz(h):
            s0, s1 = HALF[h]
            out = T.ZF if last else T["ZO%d" % (t + 1)]
            act(out[:, s0:s1], T.T3[:, s0:s1], F.Abs, "T3%d cm255" % h, "ZO%d" % h, bias=cf(23))
            if last:
                dma("Y", T.yz[:, s0:s1], out[:, s0:s1], "o_yz%d" % h, "ZO%d" % h, "")
            else:
                send("Z", t + 1, h, s0, s1, out, "ZO%d" % h)

        def conf():
            e0 = " ".join("EQ0%d" % a for a in range(4))
            e1 = " ".join("EQ1%d" % a for a in range(4))
            for c in range(16):
                o = T.bL[:, 128 + 8 * c:136 + 8 * c]
                mm(o, T.EQ0[:, c, :], T.GLT[:, 16:24], "GLT " + e0, "CT", "bL", True, c < 8)
                if c >= 8:
                    mm(o, T.EQ1[:, c - 8, :], T.GLT[:, 24:32], "GLT " + e1, "CT", "bL", False, True)

        def asum():
            if not last:
                for j in range(16):
                    mm(T.bL[:, 80:81], T.ONE[:], T.GLT[:, j:j + 1], "ONE GLT", "as0", "bL", j == 0, j == 15)

        def par():
            if not last:
                tc(T.AI[:, 0:1], T.bL[:, 80:81], "as0", "as2", "bL")
                ts(T.AI[:, 1:2], T.AI[:, 0:1], 1, None, A.bitwise_and, None, "as2", "as3")
                ts(T.THR[:, t + 1:t + 2], T.AI[:, 1:2], 2.0, float(2 * QU - 16), A.mult, A.add, "as3", "thd%d" % (t + 1))
                ts(T.THR[:, t + 5:t + 6], T.AI[:, 1:2], -2.0, 17.0 - 2 * QU, A.mult, A.add, "as3", "thb%d" % (t + 1))

        def cx():
            op("V", lambda: V.tensor_tensor_scan(T.CX[:], T.DX[:], T.bL[:, 128:256], 0.0, A.add, A.max), "DX CT", "CX", "bL")
            ts(lf(6), T.CX[:, 7::8], cf(18), None, A.is_le, None, "CX nb", "free")
            tt(lf(7), lf(6), lf(5), A.mult, "free gd", "w2")
            tt(lf(8), lf(7), T.SL[:, 16:32], A.add, "w2 b512", "off")
            tc(T.OFF[:], lf(8), "off", "OFF")

        def ml():
            tc(li(0), ML[:], mr, "mI")
            ts(li(1), li(0), 37.0, None, A.mult, None, "mI", "m37")
            if t == 0:
                later_const()

        def toL():
            tt(li(2), L(0), li(1), A.add, "uL m37", "to0", "bL")
            ts(li(3), li(2), M - 1, None, A.bitwise_and, None, "to0", "to")
            tt(lf(0), li(0), li(3), A.subtract, "mI to", "dm")

        def td():
            tt(lf(4), li(3), T.SL[:, 16:32], A.subtract, "to b512", "td")
            tt(lf(5), lf(4), T.GLT[:, 0:16], A.mult, "td GLT", "gd")

        def oP():
            act(T.bO[:, 0:B], T.OF[:], F.Copy, "OF UI", "oP", "bO")
            act(T.bO[:, B:2 * B], T.OF[:], F.Identity, "OF XQ c1184", "oK", "bO", bias=cf(16), scale=32.0)

        one = {
            "of": lambda: tc(T.OF[:], T.O16[:], "O160 O161", "OF"),
            "ui": lambda: tc(T.UI[:], T.bO[:, 0:B], "uR", "UI", "bO"),
            "uu": lambda: ts(T.UU[:], T.UI[:], W - 1, None, A.bitwise_and, None, "UI", "UU"),
            "xq": lambda: ts(T.XQ[:], T.bO[:, B:2 * B], cf(15), cf(5), A.mult, A.add, "xR cb cb2", "XQ", "bO"),
            "bit": lambda: ts(T.BIT[:], T.XQ[:], 1, None, A.bitwise_and, None, "XQ", "BIT"),
            "br": lambda: tt(T.BR[:], T.BIT[:], T.bM[:, B:2 * B], A.add, "BIT CONST", "BR", "bM"),
            "ble": lambda: ts(T.BLE[:], T.BIT[:], cf(8), cf(9), A.mult, A.add, "BIT e1 e2", "BLE"),
            "blo": lambda: ts(T.BLO[:], T.BIT[:], cf(10), cf(11), A.mult, A.add, "BIT o1 o2", "BLO"),
            "glt": lambda: ts(T.GLT[:], T.bL[:, 16:48], thdc, None, A.is_ge, None, "gL gT0 gT1 " + thd, "GLT", "bL"),
            "grep": lambda: act(T.GREP[:], T.bF[:, B:2 * B], F.Sign, "gR thb%d" % t, "GREP", "bF", bias=T.THR[:, 4 + t:5 + t]),
            "fq": lambda: tt(T.FQ[:], T.bO[:, 0:B], T.UU[:], A.mult, "oP UU", "FQ", "bO"),
            "ft": lambda: tt(T.FT[:], T.FQ[:], T.bO[:, B:2 * B], A.add, "FQ oK", "FT", "bO"),
            "fr": lambda: ts(T.FR[:], T.FT[:], 5, W - 1, A.arith_shift_right, A.bitwise_and, "FT", "FR"),
            "df": lambda: tt(T.DF[:], T.FR[:], T.bO[:, 0:B], A.subtract, "FR oP", "DF", "bO"),
            "low": lambda: ts(T.bO[:, B:2 * B], T.bL[:, B:2 * B], float(TH), None, A.is_lt, None, "use0 use1", "oK", "bL bO"),
            "ldf": lambda: tt(T.LDF[:], T.bO[:, B:2 * B], T.DF[:], A.mult, "oK DF", "LDF", "bO"),
            "wr": lambda: tt(T.MC[:, 0:M + B].indirect(T.OFF[:]), T.LDF[:], T.OF[:], A.add, "LDF OF OFF", "MC"),
            "ml": ml, "zs": zs, "c16": c16, "toL": toL, "oP": oP, "conf": conf, "td": td, "cx": cx, "as": asum, "par": par, "fl": flush}
        per = {"o16": o16, "GB": GB, "ad": ad, "prs": prs, "prv": prv_, "gw": gw, "scan": scan, "use": use, "ok": ok, "oh": oh, "vl": vl, "dl": dl,
               "sm": sm, "t1": t1, "t2": t2, "t3": t3, "sz": sz}

        def run(x):
            a, _, b = x.partition(":")
            if a in per:
                per[a](int(b))
            elif b:
                diff(int(a[1:]), int(b))
            elif a in one:
                one[a]()
            else:
                pairs(int(a[1:]))
            if t == 0 and x == "grep":
                passes()
        return run

    runs = [step(t) for t in range(T_STEPS)]
    for x in ORDER:
        if x[0] == "+":
            runs[0](x[1:])
    for t in range(T_STEPS):
        for x in ORDER:
            if x[0] != "+":
                runs[t](x)
            elif t + 1 < T_STEPS:
                runs[t + 1](x[1:])
    dma("Y", T.ymc[:], T.MC[:, 0:M], "o_ymc", "MC", "")
    need("G", [(s, cnt[s]) for s in ("V", "S", "T", "G")])
    need("G", [("l_" + x, 16) for x in LOADS] + [("o_" + x, 16) for x in OUTS])
    for t in range(1, T_STEPS):
        for h in range(2):
            for b in "mz":
                need("G", [("r%s%d%d" % (b, t, h), len(eng(prv, core))), ("s%s%d%d" % (b, t, h), len(eng(core, nxt)))])
